import numpy as np
import ml_dtypes


def mxq(x, axis, fmt="e4m3"):
    dtype, down = {"e4m3": (ml_dtypes.float8_e4m3fn, 7), "e5m2": (ml_dtypes.float8_e5m2, 14)}[fmt]
    v = np.moveaxis(np.asarray(x, np.float32).astype(ml_dtypes.bfloat16).astype(np.float64), axis, -1)
    blocks = v.reshape(v.shape[:-1] + (-1, 32))
    amax = np.abs(blocks).max(-1, keepdims=True)
    byte = np.maximum(np.where(amax > 0, np.frexp(amax)[1] - 1 + 127, 0) - down, 1)
    scale = np.exp2(byte - 127.0)
    codes = (blocks / scale).astype(np.float32).astype(dtype).astype(np.float64)
    return np.moveaxis((codes * scale).reshape(v.shape), -1, axis)


WIDE = False


def mx_kscale(k):
    if not WIDE:
        return np.ones(k)
    levels = np.array([10, -10, 5, -5, 0])
    if k % 512:
        return np.exp2(np.random.permutation(np.resize(levels, k // 32))).repeat(32)
    a = np.empty((k // 512, 16))
    for p in range(k // 512):
        a[p, :8] = np.random.permutation(np.resize(levels, 8))
        for g in range(8):
            far = levels[np.abs(levels - a[p, g]) >= 10]
            a[p, g + 8] = far[np.random.randint(len(far))]
    return np.exp2(a.ravel()).repeat(32)


def f64(x):
    return np.asarray(x).astype(np.float64)


def striped(idx):
    return np.tile(np.asarray(idx).reshape(-1, 16).T, (8, 1)).astype(np.uint16)


def unstriped(offs):
    return offs[:16].T.reshape(-1).astype(np.int64)


G, K, T, D, M = 256, 4, 1024, 1024, 256


def setup_inputs():
    n = np.random.standard_normal
    s = mx_kscale(D)[:, None]
    grid = lambda x: np.round(x * 32) / 32
    x = grid(n((D, T))) * s
    idx = np.random.randint(0, T, (G, K))
    part = np.random.randint(1, 128 // K, (G, K)) / 64.0
    return {
        "xT": x.astype(np.float32),
        "w": (n((D, M)) / np.sqrt(D) / s).astype(np.float32),
        "part": np.tile(part.reshape(-1), (128, 1)).astype(np.float32),
        "bias": (0.3 * n((M, 1))).astype(np.float32),
        "offs": striped(idx.reshape(-1)),
    }


def reference(xT, w, part, bias, offs):
    x = f64(xT)[:, unstriped(offs)]
    y = mxq(f64(w), 0, "e4m3").T @ mxq((x * f64(part)[:1]).reshape(D, G, K).sum(-1), 0, "e4m3")
    y = y + f64(bias)
    return y

@@ -1,0 +1,245 @@
+from contextlib import ExitStack
+
+import concourse.mybir as mybir
+from concourse.masks import make_identity
+
+FLOPS = 2 * 256 * 1024 * 256
+
+F32 = mybir.dt.float32
+BF16 = mybir.dt.bfloat16
+U32 = mybir.dt.uint32
+U16 = mybir.dt.uint16
+U8 = mybir.dt.uint8
+FP8X4 = mybir.dt.float8_e4m3fn_x4
+COPY = mybir.ActivationFunctionType.Copy
+IDENT = mybir.ActivationFunctionType.Identity
+ADD = mybir.AluOpType.add
+MULT = mybir.AluOpType.mult
+AXIS_X = mybir.AxisListType.X
+
+P = 128
+T = 1024
+M = 256
+G = 256
+K = 4
+PACK = 4
+GB = G // P
+HALF = T // 2
+
+
+def tile_attend_grid_bias_kernel(tc, xT, w, part, bias, offs, out):
+    nc = tc.nc
+    with ExitStack() as ctx:
+        keep = ctx.enter_context(tc.tile_pool(name="keep", bufs=1))
+        ring = ctx.enter_context(tc.tile_pool(name="ring", bufs=3))
+        tpsum = ctx.enter_context(tc.psum_pool(name="tpsum", bufs=3))
+        epsum = ctx.enter_context(tc.psum_pool(name="epsum", bufs=3))
+        opsum = ctx.enter_context(tc.psum_pool(name="opsum", bufs=2))
+
+        x = xT.rearrange("(s p t) c -> s p t c", p=P, t=PACK)
+        wv = w.rearrange("(s p t) m -> s p t m", p=P, t=PACK)
+
+        offsets = keep.tile([P, G * K // 16], U16, name="offsets")
+        nc.sync.dma_start(offsets[:], offs)
+        part_t = keep.tile([P, GB, 8], F32, name="part_t")
+        nc.scalar.dma_start(
+            out=part_t[:, :, :K], in_=part[0:1, :].rearrange("o (b g j) -> (o g) b j", b=GB, j=K)
+        )
+        bias_t = keep.tile([P, M // P], F32, name="bias_t")
+        nc.scalar.dma_start(out=bias_t[:], in_=bias.rearrange("(i m) o -> m (i o)", m=P))
+
+        pairs = [(0, 0), (0, 1), (1, 0)]
+        raw = [keep.tile([P, 2, T], F32, name=f"raw{n}") for n in range(3)]
+        packed = [keep.tile([P, T, 2], BF16, name=f"packed{n}") for n in range(3)]
+        plane = [keep.tile([P, T], F32, name=f"plane{n}") for n in range(2)]
+        part_all = keep.tile([P, G * K], F32, name="part_all")
+        w_raw = [keep.tile([P, PACK, M], F32, name=f"w_raw{s}") for s in range(2)]
+
+        def load_pair(n):
+            s, u = pairs[n]
+            for h in range(2):
+                cols = slice(h * HALF, (h + 1) * HALF)
+                nc.sync.dma_start(out=raw[n][:, :, cols], in_=x[s, :, 2 * u : 2 * u + 2, cols])
+
+        load_pair(0)
+        nc.sync.dma_start(out=part_all[:], in_=part)
+        nc.sync.dma_start(out=plane[0][:], in_=x[1, :, 2, :])
+        load_pair(1)
+        load_pair(2)
+        nc.sync.dma_start(out=plane[1][:], in_=x[1, :, 3, :])
+        for s in range(2):
+            nc.sync.dma_start(out=w_raw[s][:], in_=wv[s])
+
+        ident = keep.tile([P, P], F32, name="ident")
+        make_identity(nc, ident[:])
+
+        def cast(n, h, on_scalar):
+            cols = slice(h * HALF, (h + 1) * HALF)
+            src = raw[n][:, :, cols].rearrange("p e c -> p c e")
+            dst = packed[n][:, cols, :]
+            if on_scalar:
+                nc.scalar.activation(out=dst, in_=src, func=COPY)
+            else:
+                nc.vector.tensor_copy(out=dst, in_=src)
+
+        def list_of(b):
+            return offsets[:, b * 32 : (b + 1) * 32]
+
+        grouped = [
+            [keep.tile([P, P, PACK], BF16, align_bytes=64, name=f"grouped{s}_{b}") for b in range(GB)]
+            for s in range(2)
+        ]
+        codes = [
+            [keep.tile([P, P], U32, align_bytes=64, name=f"codes{s}_{b}") for b in range(GB)]
+            for s in range(2)
+        ]
+        scales = [
+            [keep.tile([P, P], U8, align_bytes=64, name=f"scales{s}_{b}") for b in range(GB)]
+            for s in range(2)
+        ]
+        sums = {}
+
+        def gather(n, b):
+            words = ring.tile([P, P, K], U32, name="words")
+            table = packed[n][:].rearrange("p c e -> p (c e)").bitcast(U32)
+            nc.vector.tensor_copy(
+                out=words[:].rearrange("p g j -> p (g j)"), in_=table.indirect(list_of(b))
+            )
+            turned = tpsum.tile([P, K, P], F32, name="turned")
+            for j in range(K):
+                nc.tensor.transpose(turned[:, j, :], words[:, :, j].bitcast(F32), ident[:])
+            return turned
+
+        def products(n, b, turned):
+            prod = ring.tile([P, K, 2, P], F32, name="prod")
+            for j in range(K):
+                nc.scalar.activation(
+                    out=prod[:, j],
+                    in_=turned[:, j, :].bitcast(BF16).rearrange("g (p e) -> g e p", e=2),
+                    func=COPY,
+                    scale=part_t[:, b, j : j + 1],
+                )
+            s, u = pairs[n]
+            if (s, b) not in sums:
+                sums[s, b] = epsum.tile([P, PACK, P], F32, name="sums")
+            for e in range(2):
+                for j in range(K):
+                    nc.tensor.matmul(
+                        sums[s, b][:, 2 * u + e, :],
+                        prod[:, j, e, :],
+                        ident[:],
+                        start=(j == 0),
+                        stop=(j == K - 1),
+                        is_transpose=True,
+                    )
+
+        def round_sums(s, b, ts):
+            nc.scalar.activation(
+                out=grouped[s][b][:, :, :ts],
+                in_=sums[s, b][:, :ts, :].rearrange("p t g -> p g t"),
+                func=COPY,
+            )
+
+        def plane_gather(i, b):
+            prod = ring.tile([P, P, K], F32, name="plane_prod")
+            nc.vector.tensor_tensor(
+                prod[:].rearrange("p g j -> p (g j)"),
+                plane[i][:].indirect(list_of(b)),
+                part_all[:, b * HALF : (b + 1) * HALF],
+                MULT,
+            )
+            return prod
+
+        def plane_reduce(i, b, prod):
+            with nc.allow_low_precision(reason="the sum is float32, rounded once as it is written"):
+                nc.vector.tensor_reduce(
+                    out=grouped[1][b][:, :, 2 + i], in_=prod[:], axis=AXIS_X, op=ADD
+                )
+
+        def quantize(s, b):
+            nc.vector.quantize_mx(
+                out=codes[s][b][:].bitcast(FP8X4),
+                scales=scales[s][b][:],
+                in_=grouped[s][b][:].rearrange("p g t -> p (g t)"),
+            )
+
+        cast(0, 0, True)
+        cast(0, 1, False)
+        t00 = gather(0, 0)
+        t01 = gather(0, 1)
+        products(0, 0, t00)
+        q0 = plane_gather(0, 0)
+        q1 = plane_gather(0, 1)
+        products(0, 1, t01)
+        plane_reduce(0, 0, q0)
+        plane_reduce(0, 1, q1)
+        cast(1, 0, True)
+        cast(1, 1, False)
+        t10 = gather(1, 0)
+        t11 = gather(1, 1)
+        cast(2, 0, True)
+        cast(2, 1, True)
+        products(1, 0, t10)
+        t20 = gather(2, 0)
+        products(1, 1, t11)
+        round_sums(0, 0, PACK)
+        t21 = gather(2, 1)
+        products(2, 0, t20)
+        round_sums(0, 1, PACK)
+        q2 = plane_gather(1, 0)
+
+        w_grouped = [keep.tile([P, M, PACK], BF16, align_bytes=64, name=f"w_grouped{s}") for s in range(2)]
+        w_codes = [keep.tile([P, M], U32, align_bytes=64, name=f"w_codes{s}") for s in range(2)]
+        w_scales = [keep.tile([P, M], U8, align_bytes=64, name=f"w_scales{s}") for s in range(2)]
+        for s in range(2):
+            nc.gpsimd.tensor_scalar(
+                out=w_grouped[s][:],
+                in0=w_raw[s][:].rearrange("p t m -> p m t"),
+                scalar1=1.0,
+                scalar2=0.0,
+                op0=MULT,
+                op1=ADD,
+            )
+        products(2, 1, t21)
+        round_sums(1, 0, 2)
+        q3 = plane_gather(1, 1)
+        plane_reduce(1, 0, q2)
+        quantize(0, 0)
+        quantize(0, 1)
+        round_sums(1, 1, 2)
+        for s in range(2):
+            nc.vector.quantize_mx(
+                out=w_codes[s][:].bitcast(FP8X4),
+                scales=w_scales[s][:],
+                in_=w_grouped[s][:].rearrange("p m t -> p (m t)"),
+            )
+        plane_reduce(1, 1, q3)
+        quantize(1, 0)
+        quantize(1, 1)
+
+        result = keep.tile([P, M // P, G], F32, name="result")
+        out_v = out.rearrange("(i m) g -> m i g", m=P)
+        for b in range(GB):
+            points = slice(b * P, (b + 1) * P)
+            for i in range(M // P):
+                rows = slice(i * P, (i + 1) * P)
+                acc = opsum.tile([P, P], F32, name="acc")
+                for s in range(2):
+                    nc.tensor.matmul_mx(
+                        out=acc[:],
+                        lhsT=w_codes[s][:, rows].bitcast(FP8X4),
+                        lhsT_scale=w_scales[s][:, rows],
+                        rhs=codes[s][b][:].bitcast(FP8X4),
+                        rhs_scale=scales[s][b][:],
+                        start=(s == 0),
+                        stop=(s == 1),
+                    )
+                if i == 0:
+                    nc.scalar.activation(
+                        out=result[:, i, points], in_=acc[:], func=IDENT, bias=bias_t[:, i : i + 1]
+                    )
+                else:
+                    nc.vector.tensor_scalar(
+                        out=result[:, i, points], in0=acc[:], scalar1=bias_t[:, i : i + 1], scalar2=None, op0=ADD
+                    )
+            nc.sync.dma_start(out=out_v[:, :, points], in_=result[:, :, points])

@@ -31,10 +31,9 @@ def tile_attend_grid_bias_kernel(tc, xT, w, part, bias, offs, out):
     nc = tc.nc
     with ExitStack() as ctx:
         keep = ctx.enter_context(tc.tile_pool(name="keep", bufs=1))
-        ring = ctx.enter_context(tc.tile_pool(name="ring", bufs=3))
-        tpsum = ctx.enter_context(tc.psum_pool(name="tpsum", bufs=3))
-        epsum = ctx.enter_context(tc.psum_pool(name="epsum", bufs=3))
-        opsum = ctx.enter_context(tc.psum_pool(name="opsum", bufs=2))
+        ring = ctx.enter_context(tc.tile_pool(name="ring", bufs=8))
+        banks = ctx.enter_context(tc.psum_pool(name="banks", bufs=4))
+        held = ctx.enter_context(tc.psum_pool(name="held", bufs=1))
 
         x = xT.rearrange("(s p t) c -> s p t c", p=P, t=PACK)
         wv = w.rearrange("(s p t) m -> s p t m", p=P, t=PACK)
@@ -48,27 +47,26 @@ def tile_attend_grid_bias_kernel(tc, xT, w, part, bias, offs, out):
         bias_t = keep.tile([P, M // P], F32, name="bias_t")
         nc.scalar.dma_start(out=bias_t[:], in_=bias.rearrange("(i m) o -> m (i o)", m=P))
 
-        pairs = [(0, 0), (0, 1), (1, 0)]
-        raw = [keep.tile([P, 2, T], F32, name=f"raw{n}") for n in range(3)]
-        packed = [keep.tile([P, T, 2], BF16, name=f"packed{n}") for n in range(3)]
-        plane = [keep.tile([P, T], F32, name=f"plane{n}") for n in range(2)]
-        part_all = keep.tile([P, G * K], F32, name="part_all")
+        pairs = [(0, 0), (0, 1), (1, 0), (1, 1)]
+        raw = [keep.tile([P, 2, T], F32, name=f"raw{n}") for n in range(4)]
+        packed = [keep.tile([P, T, 2], BF16, name=f"packed{n}") for n in range(4)]
         w_raw = [keep.tile([P, PACK, M], F32, name=f"w_raw{s}") for s in range(2)]
 
-        def load_pair(n):
+        def load_pair(n, pieces):
             s, u = pairs[n]
-            for h in range(2):
-                cols = slice(h * HALF, (h + 1) * HALF)
+            for h in range(pieces):
+                cols = slice(h * T // pieces, (h + 1) * T // pieces)
                 nc.sync.dma_start(out=raw[n][:, :, cols], in_=x[s, :, 2 * u : 2 * u + 2, cols])
 
-        load_pair(0)
-        nc.sync.dma_start(out=part_all[:], in_=part)
-        nc.sync.dma_start(out=plane[0][:], in_=x[1, :, 2, :])
-        load_pair(1)
-        load_pair(2)
-        nc.sync.dma_start(out=plane[1][:], in_=x[1, :, 3, :])
-        for s in range(2):
+        def load_w(s):
             nc.sync.dma_start(out=w_raw[s][:], in_=wv[s])
+
+        load_pair(0, 2)
+        load_pair(1, 2)
+        load_pair(2, 2)
+        load_pair(3, 2)
+        load_w(0)
+        load_w(1)
 
         ident = keep.tile([P, P], F32, name="ident")
         make_identity(nc, ident[:])
@@ -97,35 +95,40 @@ def tile_attend_grid_bias_kernel(tc, xT, w, part, bias, offs, out):
             [keep.tile([P, P], U8, align_bytes=64, name=f"scales{s}_{b}") for b in range(GB)]
             for s in range(2)
         ]
-        sums = {}
+        sums = [
+            [held.tile([P, PACK, P], F32, name=f"sums{s}_{b}") for b in range(GB)]
+            for s in range(2)
+        ]
 
-        def gather(n, b):
+        def gather(n, b, split=False):
             words = ring.tile([P, P, K], U32, name="words")
             table = packed[n][:].rearrange("p c e -> p (c e)").bitcast(U32)
             nc.vector.tensor_copy(
                 out=words[:].rearrange("p g j -> p (g j)"), in_=table.indirect(list_of(b))
             )
-            turned = tpsum.tile([P, K, P], F32, name="turned")
-            for j in range(K):
-                nc.tensor.transpose(turned[:, j, :], words[:, :, j].bitcast(F32), ident[:])
+            turned = []
+            for h in range(2 if split else 1):
+                bank = banks.tile([P, K, P], F32, name="bank")
+                width = K // 2 if split else K
+                for j in range(h * width, (h + 1) * width):
+                    nc.tensor.transpose(bank[:, j, :], words[:, :, j].bitcast(F32), ident[:])
+                    turned.append(bank)
             return turned
 
-        def products(n, b, turned):
+        def products(n, b, turned, engines="SSSS"):
             prod = ring.tile([P, K, 2, P], F32, name="prod")
             for j in range(K):
-                nc.scalar.activation(
-                    out=prod[:, j],
-                    in_=turned[:, j, :].bitcast(BF16).rearrange("g (p e) -> g e p", e=2),
-                    func=COPY,
-                    scale=part_t[:, b, j : j + 1],
-                )
+                src = turned[j][:, j, :].bitcast(BF16).rearrange("g (p e) -> g e p", e=2)
+                weight = part_t[:, b, j : j + 1]
+                if engines[j] == "S":
+                    nc.scalar.activation(out=prod[:, j], in_=src, func=COPY, scale=weight)
+                else:
+                    nc.vector.tensor_scalar(out=prod[:, j], in0=src, scalar1=weight, scalar2=None, op0=MULT)
             s, u = pairs[n]
-            if (s, b) not in sums:
-                sums[s, b] = epsum.tile([P, PACK, P], F32, name="sums")
             for e in range(2):
                 for j in range(K):
                     nc.tensor.matmul(
-                        sums[s, b][:, 2 * u + e, :],
+                        sums[s][b][:, 2 * u + e, :],
                         prod[:, j, e, :],
                         ident[:],
                         start=(j == 0),
@@ -133,28 +136,12 @@ def tile_attend_grid_bias_kernel(tc, xT, w, part, bias, offs, out):
                         is_transpose=True,
                     )
 
-        def round_sums(s, b, ts):
-            nc.scalar.activation(
-                out=grouped[s][b][:, :, :ts],
-                in_=sums[s, b][:, :ts, :].rearrange("p t g -> p g t"),
-                func=COPY,
-            )
-
-        def plane_gather(i, b):
-            prod = ring.tile([P, P, K], F32, name="plane_prod")
-            nc.vector.tensor_tensor(
-                prod[:].rearrange("p g j -> p (g j)"),
-                plane[i][:].indirect(list_of(b)),
-                part_all[:, b * HALF : (b + 1) * HALF],
-                MULT,
-            )
-            return prod
-
-        def plane_reduce(i, b, prod):
-            with nc.allow_low_precision(reason="the sum is float32, rounded once as it is written"):
-                nc.vector.tensor_reduce(
-                    out=grouped[1][b][:, :, 2 + i], in_=prod[:], axis=AXIS_X, op=ADD
-                )
+        def round_sums(s, b, on_scalar):
+            src = sums[s][b][:].rearrange("p t g -> p g t")
+            if on_scalar:
+                nc.scalar.activation(out=grouped[s][b][:], in_=src, func=COPY)
+            else:
+                nc.vector.tensor_copy(out=grouped[s][b][:], in_=src)
 
         def quantize(s, b):
             nc.vector.quantize_mx(
@@ -163,35 +150,11 @@ def tile_attend_grid_bias_kernel(tc, xT, w, part, bias, offs, out):
                 in_=grouped[s][b][:].rearrange("p g t -> p (g t)"),
             )
 
-        cast(0, 0, True)
-        cast(0, 1, False)
-        t00 = gather(0, 0)
-        t01 = gather(0, 1)
-        products(0, 0, t00)
-        q0 = plane_gather(0, 0)
-        q1 = plane_gather(0, 1)
-        products(0, 1, t01)
-        plane_reduce(0, 0, q0)
-        plane_reduce(0, 1, q1)
-        cast(1, 0, True)
-        cast(1, 1, False)
-        t10 = gather(1, 0)
-        t11 = gather(1, 1)
-        cast(2, 0, True)
-        cast(2, 1, True)
-        products(1, 0, t10)
-        t20 = gather(2, 0)
-        products(1, 1, t11)
-        round_sums(0, 0, PACK)
-        t21 = gather(2, 1)
-        products(2, 0, t20)
-        round_sums(0, 1, PACK)
-        q2 = plane_gather(1, 0)
-
         w_grouped = [keep.tile([P, M, PACK], BF16, align_bytes=64, name=f"w_grouped{s}") for s in range(2)]
         w_codes = [keep.tile([P, M], U32, align_bytes=64, name=f"w_codes{s}") for s in range(2)]
         w_scales = [keep.tile([P, M], U8, align_bytes=64, name=f"w_scales{s}") for s in range(2)]
-        for s in range(2):
+
+        def group_weights(s):
             nc.gpsimd.tensor_scalar(
                 out=w_grouped[s][:],
                 in0=w_raw[s][:].rearrange("p t m -> p m t"),
@@ -200,33 +163,62 @@ def tile_attend_grid_bias_kernel(tc, xT, w, part, bias, offs, out):
                 op0=MULT,
                 op1=ADD,
             )
-        products(2, 1, t21)
-        round_sums(1, 0, 2)
-        q3 = plane_gather(1, 1)
-        plane_reduce(1, 0, q2)
-        quantize(0, 0)
-        quantize(0, 1)
-        round_sums(1, 1, 2)
-        for s in range(2):
+
+        def quantize_weights(s):
             nc.vector.quantize_mx(
                 out=w_codes[s][:].bitcast(FP8X4),
                 scales=w_scales[s][:],
                 in_=w_grouped[s][:].rearrange("p m t -> p (m t)"),
             )
-        plane_reduce(1, 1, q3)
+
+        cast(0, 0, False)
+        group_weights(0)
+        group_weights(1)
+        cast(0, 1, False)
+        t01 = gather(0, 1, True)
+        t00 = gather(0, 0, True)
+        cast(1, 1, False)
+        cast(1, 0, True)
+        products(0, 1, t01, "SSSS")
+        cast(2, 0, False)
+        products(0, 0, t00, "SSSS")
+        t11 = gather(1, 1, True)
+        cast(2, 1, True)
+        t10 = gather(1, 0)
+        products(1, 1, t11, "SSSS")
+        cast(3, 0, False)
+        t20 = gather(2, 0, True)
+        cast(3, 1, True)
+        t21 = gather(2, 1, True)
+        products(1, 0, t10, "SSSS")
+        t30 = gather(3, 0)
+        t31 = gather(3, 1, True)
+        products(2, 0, t20, "SSSS")
+        products(3, 0, t30, "VVVV")
+        products(2, 1, t21, "SSSS")
+        round_sums(0, 0, False)
+        products(3, 1, t31, "SSVV")
+        quantize_weights(0)
+        round_sums(0, 1, True)
+        quantize(0, 1)
+        round_sums(1, 0, True)
+        quantize(0, 0)
+        quantize_weights(1)
+        round_sums(1, 1, True)
         quantize(1, 0)
         quantize(1, 1)
 
         result = keep.tile([P, M // P, G], F32, name="result")
         out_v = out.rearrange("(i m) g -> m i g", m=P)
-        for b in range(GB):
+
+        def multiply(b, engines):
             points = slice(b * P, (b + 1) * P)
             for i in range(M // P):
                 rows = slice(i * P, (i + 1) * P)
-                acc = opsum.tile([P, P], F32, name="acc")
+                acc = banks.tile([P, K, P], F32, name="bank")
                 for s in range(2):
                     nc.tensor.matmul_mx(
-                        out=acc[:],
+                        out=acc[:, 0, :],
                         lhsT=w_codes[s][:, rows].bitcast(FP8X4),
                         lhsT_scale=w_scales[s][:, rows],
                         rhs=codes[s][b][:].bitcast(FP8X4),
@@ -234,12 +226,15 @@ def tile_attend_grid_bias_kernel(tc, xT, w, part, bias, offs, out):
                         start=(s == 0),
                         stop=(s == 1),
                     )
-                if i == 0:
+                if engines[i] == "S":
                     nc.scalar.activation(
-                        out=result[:, i, points], in_=acc[:], func=IDENT, bias=bias_t[:, i : i + 1]
+                        out=result[:, i, points], in_=acc[:, 0, :], func=IDENT, bias=bias_t[:, i : i + 1]
                     )
                 else:
                     nc.vector.tensor_scalar(
-                        out=result[:, i, points], in0=acc[:], scalar1=bias_t[:, i : i + 1], scalar2=None, op0=ADD
+                        out=result[:, i, points], in0=acc[:, 0, :], scalar1=bias_t[:, i : i + 1], scalar2=None, op0=ADD
                     )
             nc.sync.dma_start(out=out_v[:, :, points], in_=result[:, :, points])
+
+        multiply(0, "SV")
+        multiply(1, "SV")

@@ -39,34 +39,35 @@ def tile_attend_grid_bias_kernel(tc, xT, w, part, bias, offs, out):
         wv = w.rearrange("(s p t) m -> s p t m", p=P, t=PACK)
 
         offsets = keep.tile([P, G * K // 16], U16, name="offsets")
-        nc.sync.dma_start(offsets[:], offs)
         part_t = keep.tile([P, GB, 8], F32, name="part_t")
-        nc.scalar.dma_start(
-            out=part_t[:, :, :K], in_=part[0:1, :].rearrange("o (b g j) -> (o g) b j", b=GB, j=K)
-        )
         bias_t = keep.tile([P, M // P], F32, name="bias_t")
-        nc.scalar.dma_start(out=bias_t[:], in_=bias.rearrange("(i m) o -> m (i o)", m=P))
 
         pairs = [(0, 0), (0, 1), (1, 0), (1, 1)]
         raw = [keep.tile([P, 2, T], F32, name=f"raw{n}") for n in range(4)]
         packed = [keep.tile([P, T, 2], BF16, name=f"packed{n}") for n in range(4)]
         w_raw = [keep.tile([P, PACK, M], F32, name=f"w_raw{s}") for s in range(2)]
 
-        def load_pair(n, pieces):
+        def load_half(n, h):
             s, u = pairs[n]
-            for h in range(pieces):
-                cols = slice(h * T // pieces, (h + 1) * T // pieces)
-                nc.sync.dma_start(out=raw[n][:, :, cols], in_=x[s, :, 2 * u : 2 * u + 2, cols])
+            cols = slice(h * HALF, (h + 1) * HALF)
+            nc.sync.dma_start(out=raw[n][:, :, cols], in_=x[s, :, 2 * u : 2 * u + 2, cols])
 
         def load_w(s):
             nc.sync.dma_start(out=w_raw[s][:], in_=wv[s])
 
-        load_pair(0, 2)
-        load_pair(1, 2)
-        load_pair(2, 2)
-        load_pair(3, 2)
+        load_half(1, 0)
+        nc.sync.dma_start(offsets[:], offs)
+        load_half(1, 1)
+        nc.sync.dma_start(out=part_t[:, :, :K], in_=part[0:1, :].rearrange("o (b g j) -> (o g) b j", b=GB, j=K))
+        load_half(0, 0)
+        load_half(0, 1)
+        load_half(2, 1)
+        load_half(2, 0)
         load_w(0)
+        load_half(3, 0)
+        load_half(3, 1)
         load_w(1)
+        nc.sync.dma_start(out=bias_t[:], in_=bias.rearrange("(i m) o -> m (i o)", m=P))
 
         ident = keep.tile([P, P], F32, name="ident")
         make_identity(nc, ident[:])
@@ -100,41 +101,57 @@ def tile_attend_grid_bias_kernel(tc, xT, w, part, bias, offs, out):
             for s in range(2)
         ]
 
-        def gather(n, b, split=False):
+        def gather(n, b, parts):
             words = ring.tile([P, P, K], U32, name="words")
             table = packed[n][:].rearrange("p c e -> p (c e)").bitcast(U32)
             nc.vector.tensor_copy(
                 out=words[:].rearrange("p g j -> p (g j)"), in_=table.indirect(list_of(b))
             )
-            turned = []
-            for h in range(2 if split else 1):
+            turned = {}
+            for corners in parts:
                 bank = banks.tile([P, K, P], F32, name="bank")
-                width = K // 2 if split else K
-                for j in range(h * width, (h + 1) * width):
+                for j in corners:
                     nc.tensor.transpose(bank[:, j, :], words[:, :, j].bitcast(F32), ident[:])
-                    turned.append(bank)
+                    turned[j] = bank
             return turned
 
-        def products(n, b, turned, engines="SSSS"):
-            prod = ring.tile([P, K, 2, P], F32, name="prod")
-            for j in range(K):
-                src = turned[j][:, j, :].bitcast(BF16).rearrange("g (p e) -> g e p", e=2)
-                weight = part_t[:, b, j : j + 1]
-                if engines[j] == "S":
-                    nc.scalar.activation(out=prod[:, j], in_=src, func=COPY, scale=weight)
-                else:
-                    nc.vector.tensor_scalar(out=prod[:, j], in0=src, scalar1=weight, scalar2=None, op0=MULT)
+        def scaled(n, b, turned, j):
+            return turned[j][:, j, :].bitcast(BF16).rearrange("g (p e) -> g e p", e=2), part_t[:, b, j : j + 1]
+
+        def add_up(n, b, prod, corners):
             s, u = pairs[n]
             for e in range(2):
-                for j in range(K):
+                for j in corners:
                     nc.tensor.matmul(
                         sums[s][b][:, 2 * u + e, :],
                         prod[:, j, e, :],
                         ident[:],
-                        start=(j == 0),
-                        stop=(j == K - 1),
+                        start=(j == corners[0]),
+                        stop=(j == corners[-1]),
                         is_transpose=True,
                     )
+
+        def products(n, b, turned, engines):
+            prod = ring.tile([P, K, 2, P], F32, name="prod")
+            for j in range(K):
+                src, weight = scaled(n, b, turned, j)
+                if engines[j] == "S":
+                    nc.scalar.activation(out=prod[:, j], in_=src, func=COPY, scale=weight)
+                else:
+                    nc.vector.tensor_scalar(out=prod[:, j], in0=src, scalar1=weight, scalar2=None, op0=MULT)
+            add_up(n, b, prod, range(K))
+
+        def products_chained(n, b, turned):
+            prod = ring.tile([P, K, 2, P], F32, name="prod")
+            for j in (0, 2):
+                src, weight = scaled(n, b, turned, j)
+                nc.scalar.activation(out=prod[:, j], in_=src, func=COPY, scale=weight)
+            for j in (1, 3):
+                src, weight = scaled(n, b, turned, j)
+                nc.vector.scalar_tensor_tensor(
+                    out=prod[:, j], in0=src, scalar=weight, in1=prod[:, j - 1], op0=MULT, op1=ADD
+                )
+            add_up(n, b, prod, (1, 3))
 
         def round_sums(s, b, on_scalar):
             src = sums[s][b][:].rearrange("p t g -> p g t")
@@ -171,42 +188,42 @@ def tile_attend_grid_bias_kernel(tc, xT, w, part, bias, offs, out):
                 in_=w_grouped[s][:].rearrange("p m t -> p (m t)"),
             )
 
-        cast(0, 0, False)
+        cast(1, 0, False)
+        cast(1, 1, False)
+        cast(0, 0, True)
+        t10 = gather(1, 0, [(0, 1), (2, 3)])
+        t11 = gather(1, 1, [(0, 1), (2, 3)])
+        products(1, 0, t10, "SSSS")
+        cast(0, 1, False)
+        t01 = gather(0, 1, [(0, 1), (2, 3)])
+        cast(2, 1, False)
+        products(1, 1, t11, "SSSS")
+        cast(2, 0, True)
+        t00 = gather(0, 0, [(0, 1, 2, 3)])
+        products(0, 1, t01, "SSSS")
+        cast(3, 0, True)
+        t21 = gather(2, 1, [(0, 1, 2, 3)])
+        t20 = gather(2, 0, [(0, 2), (1, 3)])
+        cast(3, 1, False)
+        products(0, 0, t00, "SSSS")
+        t31 = gather(3, 1, [(0, 1, 2, 3)])
+        products(2, 1, t21, "SSSS")
+        t30 = gather(3, 0, [(0, 1, 2, 3)])
+        products_chained(2, 0, t20)
         group_weights(0)
         group_weights(1)
-        cast(0, 1, False)
-        t01 = gather(0, 1, True)
-        t00 = gather(0, 0, True)
-        cast(1, 1, False)
-        cast(1, 0, True)
-        products(0, 1, t01, "SSSS")
-        cast(2, 0, False)
-        products(0, 0, t00, "SSSS")
-        t11 = gather(1, 1, True)
-        cast(2, 1, True)
-        t10 = gather(1, 0)
-        products(1, 1, t11, "SSSS")
-        cast(3, 0, False)
-        t20 = gather(2, 0, True)
-        cast(3, 1, True)
-        t21 = gather(2, 1, True)
-        products(1, 0, t10, "SSSS")
-        t30 = gather(3, 0)
-        t31 = gather(3, 1, True)
-        products(2, 0, t20, "SSSS")
-        products(3, 0, t30, "VVVV")
-        products(2, 1, t21, "SSSS")
-        round_sums(0, 0, False)
-        products(3, 1, t31, "SSVV")
+        products(3, 1, t31, "SSSV")
+        quantize_weights(1)
+        products(3, 0, t30, "SSVV")
         quantize_weights(0)
+        round_sums(1, 1, False)
+        quantize(1, 1)
         round_sums(0, 1, True)
         quantize(0, 1)
-        round_sums(1, 0, True)
+        round_sums(0, 0, True)
         quantize(0, 0)
-        quantize_weights(1)
-        round_sums(1, 1, True)
+        round_sums(1, 0, True)
         quantize(1, 0)
-        quantize(1, 1)
 
         result = keep.tile([P, M // P, G], F32, name="result")
         out_v = out.rearrange("(i m) g -> m i g", m=P)
@@ -236,5 +253,5 @@ def tile_attend_grid_bias_kernel(tc, xT, w, part, bias, offs, out):
                     )
             nc.sync.dma_start(out=out_v[:, :, points], in_=result[:, :, points])
 
+        multiply(1, "VV")
         multiply(0, "SV")
-        multiply(1, "SV")

@@ -3,8 +3,6 @@ from contextlib import ExitStack
 import concourse.mybir as mybir
 from concourse.masks import make_identity
 
-FLOPS = 2 * 256 * 1024 * 256
-
 F32 = mybir.dt.float32
 BF16 = mybir.dt.bfloat16
 U32 = mybir.dt.uint32
@@ -12,246 +10,241 @@ U16 = mybir.dt.uint16
 U8 = mybir.dt.uint8
 FP8X4 = mybir.dt.float8_e4m3fn_x4
 COPY = mybir.ActivationFunctionType.Copy
-IDENT = mybir.ActivationFunctionType.Identity
+IDENTITY = mybir.ActivationFunctionType.Identity
 ADD = mybir.AluOpType.add
 MULT = mybir.AluOpType.mult
-AXIS_X = mybir.AxisListType.X
 
 P = 128
+D = 1024
 T = 1024
 M = 256
 G = 256
 K = 4
 PACK = 4
-GB = G // P
+PASSES = D // (P * PACK)
+BLOCKS = G // P
+CHANNELS = M // P
 HALF = T // 2
+ENTRIES = P * K
+LIST_COLUMNS = ENTRIES // 16
+
+FLOPS = 2 * D * M * G
 
 
 def tile_attend_grid_bias_kernel(tc, xT, w, part, bias, offs, out):
     nc = tc.nc
     with ExitStack() as ctx:
         keep = ctx.enter_context(tc.tile_pool(name="keep", bufs=1))
-        ring = ctx.enter_context(tc.tile_pool(name="ring", bufs=8))
+        pieces = ctx.enter_context(tc.tile_pool(name="pieces", bufs=8))
         banks = ctx.enter_context(tc.psum_pool(name="banks", bufs=4))
         held = ctx.enter_context(tc.psum_pool(name="held", bufs=1))
 
-        x = xT.rearrange("(s p t) c -> s p t c", p=P, t=PACK)
-        wv = w.rearrange("(s p t) m -> s p t m", p=P, t=PACK)
+        x_view = xT.rearrange("(s p t) c -> s p t c", p=P, t=PACK)
+        w_view = w.rearrange("(s p t) m -> s p t m", p=P, t=PACK)
+        out_view = out.rearrange("(i m) g -> m i g", m=P)
 
+        pairs = [(s, u) for s in range(PASSES) for u in range(2)]
+        rows = [keep.tile([P, 2, T], F32, name=f"rows{n}") for n in range(len(pairs))]
+        table = [keep.tile([P, T, 2], BF16, name=f"table{n}") for n in range(len(pairs))]
+        w_rows = [keep.tile([P, PACK, M], F32, name=f"w_rows{s}") for s in range(PASSES)]
         offsets = keep.tile([P, G * K // 16], U16, name="offsets")
-        part_t = keep.tile([P, GB, 8], F32, name="part_t")
-        bias_t = keep.tile([P, M // P], F32, name="bias_t")
+        weights = keep.tile([P, BLOCKS, 8], F32, name="weights")
+        bias_cols = keep.tile([P, CHANNELS], F32, name="bias_cols")
 
-        pairs = [(0, 0), (0, 1), (1, 0), (1, 1)]
-        raw = [keep.tile([P, 2, T], F32, name=f"raw{n}") for n in range(4)]
-        packed = [keep.tile([P, T, 2], BF16, name=f"packed{n}") for n in range(4)]
-        w_raw = [keep.tile([P, PACK, M], F32, name=f"w_raw{s}") for s in range(2)]
-
-        def load_half(n, h):
+        def load_rows(n, h):
             s, u = pairs[n]
             cols = slice(h * HALF, (h + 1) * HALF)
-            nc.sync.dma_start(out=raw[n][:, :, cols], in_=x[s, :, 2 * u : 2 * u + 2, cols])
+            nc.sync.dma_start(out=rows[n][:, :, cols], in_=x_view[s, :, 2 * u : 2 * u + 2, cols])
 
-        def load_w(s):
-            nc.sync.dma_start(out=w_raw[s][:], in_=wv[s])
-
-        load_half(1, 0)
+        load_rows(0, 0)
         nc.sync.dma_start(offsets[:], offs)
-        load_half(1, 1)
-        nc.sync.dma_start(out=part_t[:, :, :K], in_=part[0:1, :].rearrange("o (b g j) -> (o g) b j", b=GB, j=K))
-        load_half(0, 0)
-        load_half(0, 1)
-        load_half(2, 1)
-        load_half(2, 0)
-        load_w(0)
-        load_half(3, 0)
-        load_half(3, 1)
-        load_w(1)
-        nc.sync.dma_start(out=bias_t[:], in_=bias.rearrange("(i m) o -> m (i o)", m=P))
+        load_rows(0, 1)
+        nc.sync.dma_start(
+            out=weights[:, :, :K], in_=part[0:1, :].rearrange("o (b g j) -> (o g) b j", b=BLOCKS, j=K)
+        )
+        for n in range(1, len(pairs)):
+            for h in range(2):
+                load_rows(n, h)
+        for s in range(PASSES):
+            nc.sync.dma_start(out=w_rows[s][:], in_=w_view[s])
+        nc.sync.dma_start(out=bias_cols[:], in_=bias.rearrange("(i m) o -> m (i o)", m=P))
 
         ident = keep.tile([P, P], F32, name="ident")
         make_identity(nc, ident[:])
 
-        def cast(n, h, on_scalar):
-            cols = slice(h * HALF, (h + 1) * HALF)
-            src = raw[n][:, :, cols].rearrange("p e c -> p c e")
-            dst = packed[n][:, cols, :]
-            if on_scalar:
-                nc.scalar.activation(out=dst, in_=src, func=COPY)
-            else:
-                nc.vector.tensor_copy(out=dst, in_=src)
-
-        def list_of(b):
-            return offsets[:, b * 32 : (b + 1) * 32]
-
-        grouped = [
-            [keep.tile([P, P, PACK], BF16, align_bytes=64, name=f"grouped{s}_{b}") for b in range(GB)]
-            for s in range(2)
+        e_values = [
+            [keep.tile([P, P, PACK], BF16, align_bytes=64, name=f"e_values{s}_{b}") for b in range(BLOCKS)]
+            for s in range(PASSES)
         ]
-        codes = [
-            [keep.tile([P, P], U32, align_bytes=64, name=f"codes{s}_{b}") for b in range(GB)]
-            for s in range(2)
+        e_codes = [
+            [keep.tile([P, P], U32, align_bytes=64, name=f"e_codes{s}_{b}") for b in range(BLOCKS)]
+            for s in range(PASSES)
         ]
-        scales = [
-            [keep.tile([P, P], U8, align_bytes=64, name=f"scales{s}_{b}") for b in range(GB)]
-            for s in range(2)
+        e_scales = [
+            [keep.tile([P, P], U8, align_bytes=64, name=f"e_scales{s}_{b}") for b in range(BLOCKS)]
+            for s in range(PASSES)
         ]
+        w_values = [keep.tile([P, M, PACK], BF16, align_bytes=64, name=f"w_values{s}") for s in range(PASSES)]
+        w_codes = [keep.tile([P, M], U32, align_bytes=64, name=f"w_codes{s}") for s in range(PASSES)]
+        w_scales = [keep.tile([P, M], U8, align_bytes=64, name=f"w_scales{s}") for s in range(PASSES)]
         sums = [
-            [held.tile([P, PACK, P], F32, name=f"sums{s}_{b}") for b in range(GB)]
-            for s in range(2)
+            [held.tile([P, PACK, P], F32, name=f"sums{s}_{b}") for b in range(BLOCKS)] for s in range(PASSES)
         ]
+        result = keep.tile([P, CHANNELS, G], F32, name="result")
 
-        def gather(n, b, parts):
-            words = ring.tile([P, P, K], U32, name="words")
-            table = packed[n][:].rearrange("p c e -> p (c e)").bitcast(U32)
+        def cast(n, h, engine):
+            cols = slice(h * HALF, (h + 1) * HALF)
+            src = rows[n][:, :, cols].rearrange("p e c -> p c e")
+            if engine == "scalar":
+                nc.scalar.activation(out=table[n][:, cols, :], in_=src, func=COPY)
+            else:
+                nc.vector.tensor_copy(out=table[n][:, cols, :], in_=src)
+
+        def gather(n, b, bank_corners):
+            words = pieces.tile([P, P, K], U32, name="words")
             nc.vector.tensor_copy(
-                out=words[:].rearrange("p g j -> p (g j)"), in_=table.indirect(list_of(b))
+                out=words[:].rearrange("p g j -> p (g j)"),
+                in_=table[n][:]
+                .rearrange("p c e -> p (c e)")
+                .bitcast(U32)
+                .indirect(offsets[:, b * LIST_COLUMNS : (b + 1) * LIST_COLUMNS]),
             )
             turned = {}
-            for corners in parts:
+            for corners in bank_corners:
                 bank = banks.tile([P, K, P], F32, name="bank")
                 for j in corners:
                     nc.tensor.transpose(bank[:, j, :], words[:, :, j].bitcast(F32), ident[:])
                     turned[j] = bank
             return turned
 
-        def scaled(n, b, turned, j):
-            return turned[j][:, j, :].bitcast(BF16).rearrange("g (p e) -> g e p", e=2), part_t[:, b, j : j + 1]
+        def corner(b, turned, j):
+            halves = turned[j][:, j, :].bitcast(BF16).rearrange("g (p e) -> g e p", e=2)
+            return halves, weights[:, b, j : j + 1]
 
-        def add_up(n, b, prod, corners):
+        def add_up(n, b, weighted, slots):
             s, u = pairs[n]
             for e in range(2):
-                for j in corners:
+                for j in slots:
                     nc.tensor.matmul(
                         sums[s][b][:, 2 * u + e, :],
-                        prod[:, j, e, :],
+                        weighted[:, j, e, :],
                         ident[:],
-                        start=(j == corners[0]),
-                        stop=(j == corners[-1]),
+                        start=(j == slots[0]),
+                        stop=(j == slots[-1]),
                         is_transpose=True,
                     )
 
-        def products(n, b, turned, engines):
-            prod = ring.tile([P, K, 2, P], F32, name="prod")
+        def weigh(n, b, turned):
+            weighted = pieces.tile([P, K, 2, P], F32, name="weighted")
             for j in range(K):
-                src, weight = scaled(n, b, turned, j)
-                if engines[j] == "S":
-                    nc.scalar.activation(out=prod[:, j], in_=src, func=COPY, scale=weight)
-                else:
-                    nc.vector.tensor_scalar(out=prod[:, j], in0=src, scalar1=weight, scalar2=None, op0=MULT)
-            add_up(n, b, prod, range(K))
+                halves, weight = corner(b, turned, j)
+                nc.scalar.activation(out=weighted[:, j], in_=halves, func=COPY, scale=weight)
+            add_up(n, b, weighted, range(K))
 
-        def products_chained(n, b, turned):
-            prod = ring.tile([P, K, 2, P], F32, name="prod")
+        def weigh_in_twos(n, b, turned):
+            weighted = pieces.tile([P, K, 2, P], F32, name="weighted")
             for j in (0, 2):
-                src, weight = scaled(n, b, turned, j)
-                nc.scalar.activation(out=prod[:, j], in_=src, func=COPY, scale=weight)
+                halves, weight = corner(b, turned, j)
+                nc.scalar.activation(out=weighted[:, j], in_=halves, func=COPY, scale=weight)
             for j in (1, 3):
-                src, weight = scaled(n, b, turned, j)
+                halves, weight = corner(b, turned, j)
                 nc.vector.scalar_tensor_tensor(
-                    out=prod[:, j], in0=src, scalar=weight, in1=prod[:, j - 1], op0=MULT, op1=ADD
+                    out=weighted[:, j], in0=halves, scalar=weight, in1=weighted[:, j - 1], op0=MULT, op1=ADD
                 )
-            add_up(n, b, prod, (1, 3))
+            add_up(n, b, weighted, (1, 3))
 
-        def round_sums(s, b, on_scalar):
-            src = sums[s][b][:].rearrange("p t g -> p g t")
-            if on_scalar:
-                nc.scalar.activation(out=grouped[s][b][:], in_=src, func=COPY)
-            else:
-                nc.vector.tensor_copy(out=grouped[s][b][:], in_=src)
+        def round_e(s, b):
+            nc.scalar.activation(out=e_values[s][b][:], in_=sums[s][b][:].rearrange("p t g -> p g t"), func=COPY)
 
-        def quantize(s, b):
+        def quantize_e(s, b):
             nc.vector.quantize_mx(
-                out=codes[s][b][:].bitcast(FP8X4),
-                scales=scales[s][b][:],
-                in_=grouped[s][b][:].rearrange("p g t -> p (g t)"),
+                out=e_codes[s][b][:].bitcast(FP8X4),
+                scales=e_scales[s][b][:],
+                in_=e_values[s][b][:].rearrange("p g t -> p (g t)"),
             )
 
-        w_grouped = [keep.tile([P, M, PACK], BF16, align_bytes=64, name=f"w_grouped{s}") for s in range(2)]
-        w_codes = [keep.tile([P, M], U32, align_bytes=64, name=f"w_codes{s}") for s in range(2)]
-        w_scales = [keep.tile([P, M], U8, align_bytes=64, name=f"w_scales{s}") for s in range(2)]
-
-        def group_weights(s):
+        def round_w(s):
             nc.gpsimd.tensor_scalar(
-                out=w_grouped[s][:],
-                in0=w_raw[s][:].rearrange("p t m -> p m t"),
+                out=w_values[s][:],
+                in0=w_rows[s][:].rearrange("p t m -> p m t"),
                 scalar1=1.0,
                 scalar2=0.0,
                 op0=MULT,
                 op1=ADD,
             )
 
-        def quantize_weights(s):
+        def quantize_w(s):
             nc.vector.quantize_mx(
                 out=w_codes[s][:].bitcast(FP8X4),
                 scales=w_scales[s][:],
-                in_=w_grouped[s][:].rearrange("p m t -> p (m t)"),
+                in_=w_values[s][:].rearrange("p m t -> p (m t)"),
             )
-
-        cast(1, 0, False)
-        cast(1, 1, False)
-        cast(0, 0, True)
-        t10 = gather(1, 0, [(0, 1), (2, 3)])
-        t11 = gather(1, 1, [(0, 1), (2, 3)])
-        products(1, 0, t10, "SSSS")
-        cast(0, 1, False)
-        t01 = gather(0, 1, [(0, 1), (2, 3)])
-        cast(2, 1, False)
-        products(1, 1, t11, "SSSS")
-        cast(2, 0, True)
-        t00 = gather(0, 0, [(0, 1, 2, 3)])
-        products(0, 1, t01, "SSSS")
-        cast(3, 0, True)
-        t21 = gather(2, 1, [(0, 1, 2, 3)])
-        t20 = gather(2, 0, [(0, 2), (1, 3)])
-        cast(3, 1, False)
-        products(0, 0, t00, "SSSS")
-        t31 = gather(3, 1, [(0, 1, 2, 3)])
-        products(2, 1, t21, "SSSS")
-        t30 = gather(3, 0, [(0, 1, 2, 3)])
-        products_chained(2, 0, t20)
-        group_weights(0)
-        group_weights(1)
-        products(3, 1, t31, "SSSV")
-        quantize_weights(1)
-        products(3, 0, t30, "SSVV")
-        quantize_weights(0)
-        round_sums(1, 1, False)
-        quantize(1, 1)
-        round_sums(0, 1, True)
-        quantize(0, 1)
-        round_sums(0, 0, True)
-        quantize(0, 0)
-        round_sums(1, 0, True)
-        quantize(1, 0)
-
-        result = keep.tile([P, M // P, G], F32, name="result")
-        out_v = out.rearrange("(i m) g -> m i g", m=P)
 
         def multiply(b, engines):
             points = slice(b * P, (b + 1) * P)
-            for i in range(M // P):
-                rows = slice(i * P, (i + 1) * P)
-                acc = banks.tile([P, K, P], F32, name="bank")
-                for s in range(2):
+            for i in range(CHANNELS):
+                channels = slice(i * P, (i + 1) * P)
+                bank = banks.tile([P, K, P], F32, name="bank")
+                for s in range(PASSES):
                     nc.tensor.matmul_mx(
-                        out=acc[:, 0, :],
-                        lhsT=w_codes[s][:, rows].bitcast(FP8X4),
-                        lhsT_scale=w_scales[s][:, rows],
-                        rhs=codes[s][b][:].bitcast(FP8X4),
-                        rhs_scale=scales[s][b][:],
+                        out=bank[:, 0, :],
+                        lhsT=w_codes[s][:, channels].bitcast(FP8X4),
+                        lhsT_scale=w_scales[s][:, channels],
+                        rhs=e_codes[s][b][:].bitcast(FP8X4),
+                        rhs_scale=e_scales[s][b][:],
                         start=(s == 0),
-                        stop=(s == 1),
+                        stop=(s == PASSES - 1),
                     )
-                if engines[i] == "S":
+                bias_col = bias_cols[:, i : i + 1]
+                if engines[i] == "scalar":
                     nc.scalar.activation(
-                        out=result[:, i, points], in_=acc[:, 0, :], func=IDENT, bias=bias_t[:, i : i + 1]
+                        out=result[:, i, points], in_=bank[:, 0, :], func=IDENTITY, bias=bias_col
                     )
                 else:
                     nc.vector.tensor_scalar(
-                        out=result[:, i, points], in0=acc[:, 0, :], scalar1=bias_t[:, i : i + 1], scalar2=None, op0=ADD
+                        out=result[:, i, points], in0=bank[:, 0, :], scalar1=bias_col, scalar2=None, op0=ADD
                     )
-            nc.sync.dma_start(out=out_v[:, :, points], in_=result[:, :, points])
+            nc.sync.dma_start(out=out_view[:, :, points], in_=result[:, :, points])
 
-        multiply(1, "VV")
-        multiply(0, "SV")
+        one_bank = [(0, 1, 2, 3)]
+        two_banks = [(0, 1), (2, 3)]
+
+        cast(0, 0, "vector")
+        cast(0, 1, "vector")
+        turned_00 = gather(0, 0, two_banks)
+        cast(1, 0, "scalar")
+        turned_01 = gather(0, 1, two_banks)
+        weigh(0, 0, turned_00)
+        cast(1, 1, "vector")
+        weigh(0, 1, turned_01)
+        for s in range(PASSES):
+            round_w(s)
+        cast(2, 0, "vector")
+        turned_10 = gather(1, 0, one_bank)
+        cast(2, 1, "scalar")
+        turned_11 = gather(1, 1, two_banks)
+        cast(3, 0, "scalar")
+        turned_20 = gather(2, 0, one_bank)
+        weigh(1, 0, turned_10)
+        cast(3, 1, "vector")
+        turned_21 = gather(2, 1, one_bank)
+        weigh(1, 1, turned_11)
+        turned_30 = gather(3, 0, one_bank)
+        turned_31 = gather(3, 1, one_bank)
+
+        weigh_in_twos(2, 0, turned_20)
+        round_e(0, 0)
+        weigh_in_twos(2, 1, turned_21)
+        weigh_in_twos(3, 0, turned_30)
+        weigh_in_twos(3, 1, turned_31)
+        round_e(0, 1)
+        quantize_e(0, 0)
+        round_e(1, 0)
+        for s in range(PASSES):
+            quantize_w(s)
+        round_e(1, 1)
+        quantize_e(1, 0)
+        quantize_e(0, 1)
+        quantize_e(1, 1)
+        multiply(0, ("vector", "vector"))
+        multiply(1, ("scalar", "vector"))

from contextlib import ExitStack

import concourse.mybir as mybir
from concourse.masks import make_identity

F32 = mybir.dt.float32
BF16 = mybir.dt.bfloat16
U32 = mybir.dt.uint32
U16 = mybir.dt.uint16
U8 = mybir.dt.uint8
FP8X4 = mybir.dt.float8_e4m3fn_x4
COPY = mybir.ActivationFunctionType.Copy
IDENTITY = mybir.ActivationFunctionType.Identity
ADD = mybir.AluOpType.add
MULT = mybir.AluOpType.mult

P = 128
D = 1024
T = 1024
M = 256
G = 256
K = 4
PACK = 4
PASSES = D // (P * PACK)
BLOCKS = G // P
CHANNELS = M // P
HALF = T // 2
ENTRIES = P * K
LIST_COLUMNS = ENTRIES // 16

FLOPS = 2 * D * M * G


def tile_attend_grid_bias_kernel(tc, xT, w, part, bias, offs, out):
    nc = tc.nc
    with ExitStack() as ctx:
        keep = ctx.enter_context(tc.tile_pool(name="keep", bufs=1))
        pieces = ctx.enter_context(tc.tile_pool(name="pieces", bufs=8))
        banks = ctx.enter_context(tc.psum_pool(name="banks", bufs=4))
        held = ctx.enter_context(tc.psum_pool(name="held", bufs=1))

        x_view = xT.rearrange("(s p t) c -> s p t c", p=P, t=PACK)
        w_view = w.rearrange("(s p t) m -> s p t m", p=P, t=PACK)
        out_view = out.rearrange("(i m) g -> m i g", m=P)

        pairs = [(s, u) for s in range(PASSES) for u in range(2)]
        rows = [keep.tile([P, 2, T], F32, name=f"rows{n}") for n in range(len(pairs))]
        table = [keep.tile([P, T, 2], BF16, name=f"table{n}") for n in range(len(pairs))]
        w_rows = [keep.tile([P, PACK, M], F32, name=f"w_rows{s}") for s in range(PASSES)]
        offsets = keep.tile([P, G * K // 16], U16, name="offsets")
        weights = keep.tile([P, BLOCKS, 8], F32, name="weights")
        bias_cols = keep.tile([P, CHANNELS], F32, name="bias_cols")

        def load_rows(n, h):
            s, u = pairs[n]
            cols = slice(h * HALF, (h + 1) * HALF)
            nc.sync.dma_start(out=rows[n][:, :, cols], in_=x_view[s, :, 2 * u : 2 * u + 2, cols])

        load_rows(0, 0)
        nc.sync.dma_start(offsets[:], offs)
        load_rows(0, 1)
        nc.sync.dma_start(
            out=weights[:, :, :K], in_=part[0:1, :].rearrange("o (b g j) -> (o g) b j", b=BLOCKS, j=K)
        )
        for n in range(1, len(pairs)):
            for h in range(2):
                load_rows(n, h)
        for s in range(PASSES):
            nc.sync.dma_start(out=w_rows[s][:], in_=w_view[s])
        nc.sync.dma_start(out=bias_cols[:], in_=bias.rearrange("(i m) o -> m (i o)", m=P))

        ident = keep.tile([P, P], F32, name="ident")
        make_identity(nc, ident[:])

        e_values = [
            [keep.tile([P, P, PACK], BF16, align_bytes=64, name=f"e_values{s}_{b}") for b in range(BLOCKS)]
            for s in range(PASSES)
        ]
        e_codes = [
            [keep.tile([P, P], U32, align_bytes=64, name=f"e_codes{s}_{b}") for b in range(BLOCKS)]
            for s in range(PASSES)
        ]
        e_scales = [
            [keep.tile([P, P], U8, align_bytes=64, name=f"e_scales{s}_{b}") for b in range(BLOCKS)]
            for s in range(PASSES)
        ]
        w_values = [keep.tile([P, M, PACK], BF16, align_bytes=64, name=f"w_values{s}") for s in range(PASSES)]
        w_codes = [keep.tile([P, M], U32, align_bytes=64, name=f"w_codes{s}") for s in range(PASSES)]
        w_scales = [keep.tile([P, M], U8, align_bytes=64, name=f"w_scales{s}") for s in range(PASSES)]
        sums = [
            [held.tile([P, PACK, P], F32, name=f"sums{s}_{b}") for b in range(BLOCKS)] for s in range(PASSES)
        ]
        result = keep.tile([P, CHANNELS, G], F32, name="result")

        def cast(n, h, engine):
            cols = slice(h * HALF, (h + 1) * HALF)
            src = rows[n][:, :, cols].rearrange("p e c -> p c e")
            if engine == "scalar":
                nc.scalar.activation(out=table[n][:, cols, :], in_=src, func=COPY)
            else:
                nc.vector.tensor_copy(out=table[n][:, cols, :], in_=src)

        def gather(n, b, bank_corners):
            words = pieces.tile([P, P, K], U32, name="words")
            nc.vector.tensor_copy(
                out=words[:].rearrange("p g j -> p (g j)"),
                in_=table[n][:]
                .rearrange("p c e -> p (c e)")
                .bitcast(U32)
                .indirect(offsets[:, b * LIST_COLUMNS : (b + 1) * LIST_COLUMNS]),
            )
            turned = {}
            for corners in bank_corners:
                bank = banks.tile([P, K, P], F32, name="bank")
                for j in corners:
                    nc.tensor.transpose(bank[:, j, :], words[:, :, j].bitcast(F32), ident[:])
                    turned[j] = bank
            return turned

        def corner(b, turned, j):
            halves = turned[j][:, j, :].bitcast(BF16).rearrange("g (p e) -> g e p", e=2)
            return halves, weights[:, b, j : j + 1]

        def add_up(n, b, weighted, slots):
            s, u = pairs[n]
            for e in range(2):
                for j in slots:
                    nc.tensor.matmul(
                        sums[s][b][:, 2 * u + e, :],
                        weighted[:, j, e, :],
                        ident[:],
                        start=(j == slots[0]),
                        stop=(j == slots[-1]),
                        is_transpose=True,
                    )

        def weigh(n, b, turned):
            weighted = pieces.tile([P, K, 2, P], F32, name="weighted")
            for j in range(K):
                halves, weight = corner(b, turned, j)
                nc.scalar.activation(out=weighted[:, j], in_=halves, func=COPY, scale=weight)
            add_up(n, b, weighted, range(K))

        def weigh_in_twos(n, b, turned):
            weighted = pieces.tile([P, K, 2, P], F32, name="weighted")
            for j in (0, 2):
                halves, weight = corner(b, turned, j)
                nc.scalar.activation(out=weighted[:, j], in_=halves, func=COPY, scale=weight)
            for j in (1, 3):
                halves, weight = corner(b, turned, j)
                nc.vector.scalar_tensor_tensor(
                    out=weighted[:, j], in0=halves, scalar=weight, in1=weighted[:, j - 1], op0=MULT, op1=ADD
                )
            add_up(n, b, weighted, (1, 3))

        def round_e(s, b):
            nc.scalar.activation(out=e_values[s][b][:], in_=sums[s][b][:].rearrange("p t g -> p g t"), func=COPY)

        def quantize_e(s, b):
            nc.vector.quantize_mx(
                out=e_codes[s][b][:].bitcast(FP8X4),
                scales=e_scales[s][b][:],
                in_=e_values[s][b][:].rearrange("p g t -> p (g t)"),
            )

        def round_w(s):
            nc.gpsimd.tensor_scalar(
                out=w_values[s][:],
                in0=w_rows[s][:].rearrange("p t m -> p m t"),
                scalar1=1.0,
                scalar2=0.0,
                op0=MULT,
                op1=ADD,
            )

        def quantize_w(s):
            nc.vector.quantize_mx(
                out=w_codes[s][:].bitcast(FP8X4),
                scales=w_scales[s][:],
                in_=w_values[s][:].rearrange("p m t -> p (m t)"),
            )

        def multiply(b, engines):
            points = slice(b * P, (b + 1) * P)
            for i in range(CHANNELS):
                channels = slice(i * P, (i + 1) * P)
                bank = banks.tile([P, K, P], F32, name="bank")
                for s in range(PASSES):
                    nc.tensor.matmul_mx(
                        out=bank[:, 0, :],
                        lhsT=w_codes[s][:, channels].bitcast(FP8X4),
                        lhsT_scale=w_scales[s][:, channels],
                        rhs=e_codes[s][b][:].bitcast(FP8X4),
                        rhs_scale=e_scales[s][b][:],
                        start=(s == 0),
                        stop=(s == PASSES - 1),
                    )
                bias_col = bias_cols[:, i : i + 1]
                if engines[i] == "scalar":
                    nc.scalar.activation(
                        out=result[:, i, points], in_=bank[:, 0, :], func=IDENTITY, bias=bias_col
                    )
                else:
                    nc.vector.tensor_scalar(
                        out=result[:, i, points], in0=bank[:, 0, :], scalar1=bias_col, scalar2=None, op0=ADD
                    )
            nc.sync.dma_start(out=out_view[:, :, points], in_=result[:, :, points])

        one_bank = [(0, 1, 2, 3)]
        two_banks = [(0, 1), (2, 3)]

        cast(0, 0, "vector")
        cast(0, 1, "vector")
        turned_00 = gather(0, 0, two_banks)
        cast(1, 0, "scalar")
        turned_01 = gather(0, 1, two_banks)
        weigh(0, 0, turned_00)
        cast(1, 1, "vector")
        weigh(0, 1, turned_01)
        for s in range(PASSES):
            round_w(s)
        cast(2, 0, "vector")
        turned_10 = gather(1, 0, one_bank)
        cast(2, 1, "scalar")
        turned_11 = gather(1, 1, two_banks)
        cast(3, 0, "scalar")
        turned_20 = gather(2, 0, one_bank)
        weigh(1, 0, turned_10)
        cast(3, 1, "vector")
        turned_21 = gather(2, 1, one_bank)
        weigh(1, 1, turned_11)
        turned_30 = gather(3, 0, one_bank)
        turned_31 = gather(3, 1, one_bank)

        weigh_in_twos(2, 0, turned_20)
        round_e(0, 0)
        weigh_in_twos(2, 1, turned_21)
        weigh_in_twos(3, 0, turned_30)
        weigh_in_twos(3, 1, turned_31)
        round_e(0, 1)
        quantize_e(0, 0)
        round_e(1, 0)
        for s in range(PASSES):
            quantize_w(s)
        round_e(1, 1)
        quantize_e(1, 0)
        quantize_e(0, 1)
        quantize_e(1, 1)
        multiply(0, ("vector", "vector"))
        multiply(1, ("scalar", "vector"))
